import numpy as np
import ml_dtypes


def mxq(x, axis, fmt="e4m3"):
    dtype, down = {"e4m3": (ml_dtypes.float8_e4m3fn, 7), "e5m2": (ml_dtypes.float8_e5m2, 14)}[fmt]
    v = np.moveaxis(np.asarray(x, np.float32).astype(ml_dtypes.bfloat16).astype(np.float64), axis, -1)
    blocks = v.reshape(v.shape[:-1] + (-1, 32))
    amax = np.abs(blocks).max(-1, keepdims=True)
    byte = np.maximum(np.where(amax > 0, np.frexp(amax)[1] - 1 + 127, 0) - down, 1)
    scale = np.exp2(byte - 127.0)
    codes = (blocks / scale).astype(np.float32).astype(dtype).astype(np.float64)
    return np.moveaxis((codes * scale).reshape(v.shape), -1, axis)


WIDE = False


def mx_kscale(k):
    if not WIDE:
        return np.ones(k)
    levels = np.array([10, -10, 5, -5, 0])
    if k % 512:
        return np.exp2(np.random.permutation(np.resize(levels, k // 32))).repeat(32)
    a = np.empty((k // 512, 16))
    for p in range(k // 512):
        a[p, :8] = np.random.permutation(np.resize(levels, 8))
        for g in range(8):
            far = levels[np.abs(levels - a[p, g]) >= 10]
            a[p, g + 8] = far[np.random.randint(len(far))]
    return np.exp2(a.ravel()).repeat(32)


def f64(x):
    return np.asarray(x).astype(np.float64)


def striped(idx):
    return np.tile(idx.reshape(-1, 16).T, (8, 1)).astype(np.uint16)


def unstriped(offs):
    return offs[:16].T.reshape(-1).astype(np.int64)


def striped8(idx):
    return np.concatenate([x.reshape(-1, 16).T for x in idx]).astype(np.uint16)


def runs(offs, k):
    lists = np.stack([offs[16 * r : 16 * r + 16].T.reshape(-1) for r in range(8)]).astype(np.int64)
    return lists[np.arange(k) % 512 // 64]


def pack_weight(w):
    k, n = w.shape
    w = f64(np.asarray(w, np.float32).astype(ml_dtypes.bfloat16)).reshape(k // 32, 32, n)
    amax = np.abs(w).max(1)
    byte = np.clip(np.where(amax > 0, np.frexp(amax)[1] - 1 + 127 - 7, 1), 1, 254)
    scaled = (w * np.exp2(127.0 - byte)[:, None, :]).reshape(k, n).astype(np.float32)
    words = np.ascontiguousarray(scaled.reshape(k // 512, 128, 4, n).transpose(0, 1, 3, 2)).astype(ml_dtypes.float8_e4m3fn).view(np.uint8)
    return words, np.ascontiguousarray(byte.astype(np.uint8).reshape(k // 512, 16, n))


def unpack_weight(words, scales):
    g, p, n, _ = words.shape
    vals = np.ascontiguousarray(words).view(ml_dtypes.float8_e4m3fn).astype(np.float64) * np.repeat(np.exp2(scales.astype(np.float64) - 127.0), 8, axis=1)[..., None]
    return vals.transpose(0, 1, 3, 2).reshape(g * 512, n)


E2M1 = np.array([0.0, 0.5, 1.0, 1.5, 2.0, 3.0, 4.0, 6.0, -0.0, -0.5, -1.0, -1.5, -2.0, -3.0, -4.0, -6.0])


def pack_fp4(w):
    k, n = w.shape
    w = f64(np.asarray(w, np.float32).astype(ml_dtypes.bfloat16)).reshape(k // 32, 32, n)
    amax = np.abs(w).max(1)
    mant, ex = np.frexp(amax / 6.0)
    byte = np.clip(np.where(amax > 0, np.where(mant > 0.5, ex, ex - 1) + 127, 1), 1, 254)
    scaled = (w * np.exp2(127.0 - byte)[:, None, :]).reshape(k, n).astype(np.float32)
    c = np.ascontiguousarray(scaled.reshape(k // 512, 128, 4, n).transpose(0, 1, 3, 2)).astype(ml_dtypes.float4_e2m1fn).view(np.uint8) & 0xF
    words = (c[..., 0::2] | (c[..., 1::2] << 4)).reshape(k // 512, 128, 2 * n)
    return np.ascontiguousarray(words), np.ascontiguousarray(byte.astype(np.uint8).reshape(k // 512, 16, n))


def unpack_fp4(words, scales):
    g, _, n = scales.shape
    words = np.ascontiguousarray(words).reshape(g, 128, n, 2)
    nib = np.empty((g, 128, n, 4), np.uint8)
    nib[..., 0::2] = words & 0xF
    nib[..., 1::2] = words >> 4
    vals = E2M1[nib] * np.repeat(np.exp2(scales.astype(np.float64) - 127.0), 8, axis=1)[..., None]
    return vals.transpose(0, 1, 3, 2).reshape(g * 512, n)


def planes(y):
    n, m = y.shape
    v = y.astype(np.float32).astype(ml_dtypes.bfloat16).astype(np.float64).reshape(n // 32, 32, m)
    top = np.abs(v).max(1)
    byte = np.clip(np.where(top > 0, np.frexp(top)[1] - 1 + 127 - 7, 1), 1, 254)
    codes = (v * np.exp2(127.0 - byte)[:, None, :]).reshape(n, m).astype(np.float32).astype(ml_dtypes.float8_e4m3fn).view(np.uint8)
    words = codes.reshape(n // 512, 128, 4, m).transpose(0, 1, 3, 2)
    return np.ascontiguousarray(words), np.ascontiguousarray(byte.astype(np.uint8).reshape(n // 512, 16, m))


K, T, S, H, C = 512, 2048, 512, 512, 512


def setup_inputs():
    n = np.random.standard_normal
    s = mx_kscale(K)[:, None]
    packed_xT = pack_weight(n((K, T)) * s)
    packed_w1 = pack_fp4(n((K, H)) / np.sqrt(K) / s)
    return {
        "x_words": packed_xT[0],
        "x_scales": packed_xT[1],
        "w1_words": packed_w1[0],
        "w1_scales": packed_w1[1],
        "gs": (np.random.uniform(0.5, 1.5, (K, 1)) / s).astype(np.float32),
        "wb": (n((K, S)) / np.sqrt(K) / s).astype(np.float32),
        "offs": striped(np.random.permutation(T)[:S]),
        "n1": striped8(np.stack([np.random.permutation(S) for _ in range(8)])),
        "n2": striped8(np.stack([np.random.permutation(S) for _ in range(8)])),
        "cand": striped(np.random.permutation(T)[:C]),
        "cb": striped(np.random.permutation(T)[:C]),
        "n3": striped(np.random.permutation(S)),
        "n4": striped(np.random.permutation(S)),
    }


def reference(x_words, x_scales, w1_words, w1_scales, gs, wb, offs, n1, n2, cand, cb, n3, n4):
    x_cand = unpack_weight(x_words, x_scales)[:, unstriped(cand)]
    xq = unpack_weight(x_words, x_scales)[:, unstriped(offs)]
    y = unpack_fp4(w1_words, w1_scales).T @ xq
    pa = y[np.arange(H)[:, None], runs(n1, H)]
    pb = y[np.arange(H)[:, None], runs(n2, H)]
    mu = 0.3125 * (y + pa + pb)
    z = f64(gs) * ((y - mu) / (np.sqrt((pa - mu) ** 2 + (pb - mu) ** 2 + 0.25)))
    a = 0.0625 * ((x_cand.T @ mxq(z, 0, "e4m3")))
    x_cb = unpack_weight(x_words, x_scales)[:, unstriped(cb)]
    b = x_cb.T @ mxq(f64(wb), 0, "e4m3")
    out_0 = (a - a[:, unstriped(n3)]) / (np.abs(b) + np.abs(b[:, unstriped(n4)]) + 0.5)
    return (out_0,) + planes(out_0)

@@ -1,0 +1,319 @@
+from contextlib import ExitStack
+
+import concourse.mybir as mybir
+from concourse.masks import make_identity
+
+F32 = mybir.dt.float32
+BF16 = mybir.dt.bfloat16
+I32 = mybir.dt.int32
+U32 = mybir.dt.uint32
+U16 = mybir.dt.uint16
+U8 = mybir.dt.uint8
+FP8X4 = mybir.dt.float8_e4m3fn_x4
+FP4X4 = mybir.dt.float4_e2m1fn_x4
+ACT = mybir.ActivationFunctionType
+ALU = mybir.AluOpType
+
+P = 128
+PACK = 4
+TOKENS = 2048
+S = 512
+HALF = 256
+BLK = 128
+LIST_COLS = S // 16
+FLOPS = 3 * 2 * 512 * 512 * 512
+
+
+def tile_picked_cdswnormbstd_none_po_kernel(
+    tc, x_words, x_scales, w1_words, w1_scales, gs, wb, offs, n1, n2, cand, cb, n3, n4, out_0, out_1, out_2
+):
+    nc = tc.nc
+    with ExitStack() as ctx:
+        keep = ctx.enter_context(tc.tile_pool(name="keep", bufs=1))
+        psum = ctx.enter_context(tc.psum_pool(name="psum", bufs=1))
+
+        def sb(name, shape, dtype):
+            return keep.tile(shape, dtype, name=name, align_bytes=64)
+
+        bank = [psum.tile([P, S], F32, name="bank%d" % i) for i in range(8)]
+
+        lists = {}
+
+        def load_list(name, src):
+            lists[name] = sb("list_" + name, [P, LIST_COLS], U16)
+            nc.sync.dma_start(lists[name][:], src)
+
+        def entries(name, first, count):
+            return lists[name][:, first // 16 : (first + count) // 16]
+
+        def load_scale_rows(dst, src, queues):
+            for q in range(4):
+                queues[q].dma_start(dst[32 * q : 32 * q + 4, :].bitcast(I32), src[0, 4 * q : 4 * q + 4, :].bitcast(I32))
+
+        def weave(engine_copy, dst, planes):
+            engine_copy(
+                out=dst[:].rearrange("p (c i) t -> p c t i", i=4),
+                in_=planes.rearrange("p t (c i) -> p c t i", i=4),
+            )
+
+        def quantise(codes, scales, woven):
+            nc.vector.quantize_mx(out=codes.bitcast(FP8X4), scales=scales, in_=woven[:].rearrange("p j t -> p (j t)"))
+
+        def transpose_sum(dst, first, second):
+            nc.tensor.matmul(dst, lhsT=first, rhs=ident[:], is_transpose=True, start=True, stop=False)
+            nc.tensor.matmul(dst, lhsT=second, rhs=ident[:], is_transpose=True, start=False, stop=True)
+
+        def block(k):
+            return slice(BLK * k, BLK * (k + 1))
+
+        xs = sb("xs", [P, TOKENS], U8)
+        xw = sb("xw", [P, TOKENS], U32)
+        w1w_raw = sb("w1w_raw", [P, 2 * S], U8)
+        w1s_raw = sb("w1s_raw", [P, S], U8)
+        nc.vector.memset(xs[:].bitcast(I32), 0)
+        nc.gpsimd.memset(w1s_raw[:].bitcast(I32), 0)
+        load_list("offs", offs)
+        nc.sync.dma_start(w1w_raw[:].bitcast(I32), w1_words[0].bitcast(I32))
+        load_scale_rows(xs, x_scales, [nc.sync] * 4)
+        nc.sync.dma_start(xw[:].bitcast(I32), x_words[0].rearrange("p c r -> p (c r)").bitcast(I32))
+        load_scale_rows(w1s_raw, w1_scales, [nc.gpsimd, nc.gpsimd, nc.sync, nc.sync])
+        load_list("n1", n1)
+        load_list("n2", n2)
+        wb_raw = [sb("wb_raw%d" % h, [P, PACK, HALF], F32) for h in range(2)]
+        wb_rows = wb.rearrange("(p t) j -> p t j", t=PACK)
+        nc.sync.dma_start(wb_raw[0][:], wb_rows[:, :, 0:HALF])
+        nc.sync.dma_start(wb_raw[1][:], wb_rows[:, :, HALF:S])
+        gain = sb("gain", [P, PACK], F32)
+        nc.sync.dma_start(gain[:], gs.rearrange("(p t) o -> p (t o)", t=PACK))
+        load_list("cb", cb)
+        load_list("cand", cand)
+        load_list("n4", n4)
+        load_list("n3", n3)
+
+
+        w1w = sb("w1w", [P, 2 * S], U8)
+        w1s = sb("w1s", [P, S], U8)
+        nc.vector.tensor_copy(
+            out=w1w[:].rearrange("p (t c i b) -> p c t i b", t=PACK, i=8, b=2),
+            in_=w1w_raw[:].rearrange("p (c i t b) -> p c t i b", t=PACK, i=8, b=2),
+        )
+
+        def deal_bytes(engine, dst, src):
+            engine.tensor_copy(
+                out=dst[:].rearrange("p (t c i) -> p c t i", t=PACK, i=16),
+                in_=src[:].rearrange("p (c i t) -> p c t i", t=PACK, i=16),
+            )
+
+        deal_bytes(nc.gpsimd, w1s, w1s_raw)
+        xq_s = [sb("xq_s%d" % h, [P, HALF], U8) for h in range(2)]
+        xq_w = [sb("xq_w%d" % h, [P, HALF], U32) for h in range(2)]
+        for h in range(2):
+            nc.vector.tensor_copy(out=xq_s[h][:], in_=xs[:].indirect(entries("offs", HALF * h, HALF)))
+            nc.vector.tensor_copy(out=xq_w[h][:], in_=xw[:].indirect(entries("offs", HALF * h, HALF)))
+
+        for pair in range(2):
+            for h in range(2):
+                for t in (2 * pair, 2 * pair + 1):
+                    nc.tensor.matmul_mx(
+                        out=bank[t][:, HALF * h : HALF * (h + 1)],
+                        lhsT=w1w[:, 2 * BLK * t : 2 * BLK * (t + 1)].bitcast(FP4X4),
+                        lhsT_scale=w1s[:, block(t)],
+                        rhs=xq_w[h][:].bitcast(FP8X4),
+                        rhs_scale=xq_s[h][:],
+                        start=True,
+                        stop=True,
+                    )
+
+        ident = sb("ident", [P, P], F32)
+        make_identity(nc, ident[:])
+
+        wb_woven = [sb("wb_woven%d" % h, [P, HALF, PACK], BF16) for h in range(2)]
+
+        Y_SCALE = -25.0 / 48.0
+        yw = [sb("yw%d" % t, [P, S], F32) for t in range(PACK)]
+        nc.scalar.activation(out=yw[0][:], in_=bank[0][:], func=ACT.Copy, scale=Y_SCALE)
+        for t in range(1, PACK):
+            nc.vector.tensor_scalar(out=yw[t][:], in0=bank[t][:], scalar1=Y_SCALE, scalar2=None, op0=ALU.mult)
+
+        def pick_stationary(name):
+            words = sb(name + "_gw", [P, S], U32)
+            scales = sb(name + "_gs", [P, S], U8)
+            nc.vector.tensor_copy(out=words[:], in_=xw[:].indirect(lists[name][:]))
+            nc.vector.tensor_copy(out=scales[:], in_=xs[:].indirect(lists[name][:]))
+            dealt_w = sb(name + "_w", [P, S], U32)
+            dealt_s = sb(name + "_s", [P, S], U8)
+            nc.vector.tensor_copy(
+                out=dealt_w[:].bitcast(I32).rearrange("p (t c i) -> p c t i", t=PACK, i=4),
+                in_=words[:].bitcast(I32).rearrange("p (c i t) -> p c t i", t=PACK, i=4),
+            )
+            deal_bytes(nc.vector, dealt_s, scales)
+            return dealt_w, dealt_s
+
+        pa = [sb("pa%d" % i, [P, 2, HALF], F32) for i in range(2)]
+        nb = [sb("nb%d" % i, [P, 2, HALF], F32) for i in range(2)]
+        us = [sb("us%d" % i, [P, 2, HALF], F32) for i in range(2)]
+        sq = [sb("sq%d" % i, [P, 2 * S], F32) for i in range(2)]
+        rs = [sb("rs%d" % i, [P, 2, HALF], F32) for i in range(2)]
+        d0 = [sb("d0%d" % i, [P, 2, HALF], F32) for i in range(2)]
+        z_planes = [sb("z_planes%d" % h, [P, PACK, HALF], F32) for h in range(2)]
+        z_woven = [sb("z_woven%d" % h, [P, HALF, PACK], BF16) for h in range(2)]
+        z_w = [sb("z_w%d" % h, [P, HALF], U32) for h in range(2)]
+        z_s = [sb("z_s%d" % h, [P, HALF], U8) for h in range(2)]
+        a_bank = [bank[6], bank[7], bank[4], bank[5]]
+        aw = sb("aw", [P, PACK, S], F32)
+
+        def fetch(u):
+            h, pair = divmod(u, 2)
+            for i in range(2):
+                window = yw[2 * pair + i]
+                nc.scalar.activation(out=pa[pair][:, i, :], in_=window[:].indirect(entries("n1", HALF * h, HALF)), func=ACT.Copy, scale=-0.6)
+                nc.scalar.activation(out=nb[pair][:, i, :], in_=window[:].indirect(entries("n2", HALF * h, HALF)), func=ACT.Copy, scale=0.6)
+
+        def sums(u):
+            h, pair = divmod(u, 2)
+            nc.vector.tensor_tensor(out=us[pair][:], in0=pa[pair][:], in1=nb[pair][:], op=ALU.subtract)
+            for k in range(4):
+                i, jb = divmod(k, 2)
+                transpose_sum(bank[2 * pair][:, block(k)], pa[pair][:, i, block(jb)], nb[pair][:, i, block(jb)])
+            for k in range(4):
+                i, jb = divmod(k, 2)
+                transpose_sum(bank[2 * pair + 1][:, block(k)], yw[2 * pair + i][:, block(2 * h + jb)], us[pair][:, i, block(jb)])
+            for i in range(2):
+                nc.vector.scalar_tensor_tensor(
+                    out=d0[pair][:, i, :], in0=yw[2 * pair + i][:, HALF * h : HALF * (h + 1)], scalar=-1.32,
+                    in1=us[pair][:, i, :], op0=ALU.mult, op1=ALU.subtract,
+                )
+
+        def squares(u):
+            pair = u % 2
+            nc.scalar.activation(out=sq[pair][:, 0:S], in_=bank[2 * pair][:], func=ACT.Square, scale=3.2)
+            nc.scalar.activation(out=sq[pair][:, S : 2 * S], in_=bank[2 * pair + 1][:], func=ACT.Square, scale=1.2)
+            for k in range(4):
+                transpose_sum(bank[4 + pair][:, block(k)], sq[pair][:, block(k)], sq[pair][:, block(4 + k)])
+
+        def normalise(u):
+            h, pair = divmod(u, 2)
+            nc.scalar.activation(
+                out=rs[pair][:].rearrange("p i j -> p (i j)"), in_=bank[4 + pair][:],
+                func=ACT.Abs_reciprocal_sqrt, scale=0.5, bias=0.25,
+            )
+            for i in range(2):
+                t = 2 * pair + i
+                nc.vector.scalar_tensor_tensor(
+                    out=z_planes[h][:, t, :], in0=d0[pair][:, i, :], scalar=gain[:, t : t + 1],
+                    in1=rs[pair][:, i, :], op0=ALU.mult, op1=ALU.mult,
+                )
+
+        def scores(h):
+            weave(nc.vector.tensor_copy, z_woven[h], z_planes[h][:])
+            quantise(z_w[h][:], z_s[h][:], z_woven[h])
+            for c in range(2):
+                for t in range(PACK):
+                    nc.tensor.matmul_mx(
+                        out=a_bank[2 * h + c][:, block(t)],
+                        lhsT=cand_w[:, block(t)].bitcast(FP8X4),
+                        lhsT_scale=cand_s[:, block(t)],
+                        rhs=z_w[h][:, block(c)].bitcast(FP8X4),
+                        rhs_scale=z_s[h][:, block(c)],
+                        start=True,
+                        stop=True,
+                    )
+                nc.vector.tensor_scalar(
+                    out=aw[:, :, block(2 * h + c)], in0=a_bank[2 * h + c][:].rearrange("p (t j) -> p t j", t=PACK),
+                    scalar1=0.0625, scalar2=None, op0=ALU.mult,
+                )
+
+        wb_w = sb("wb_w", [P, S], U32)
+        wb_s = sb("wb_s", [P, S], U8)
+        ab = sb("ab", [P, PACK, S], F32)
+
+        def project(t):
+            nc.tensor.matmul_mx(
+                out=bank[6 + t % 2][:], lhsT=cb_w[:, block(t)].bitcast(FP8X4), lhsT_scale=cb_s[:, block(t)],
+                rhs=wb_w[:].bitcast(FP8X4), rhs_scale=wb_s[:], start=True, stop=True,
+            )
+            nc.scalar.activation(out=ab[:, t, :], in_=bank[6 + t % 2][:], func=ACT.Abs)
+
+        fetch(0)
+        fetch(1)
+        sums(0)
+        squares(0)
+        fetch(2)
+        sums(1)
+        normalise(0)
+        squares(1)
+        fetch(3)
+        sums(2)
+        normalise(1)
+        sums(3)
+        squares(2)
+        squares(3)
+        normalise(2)
+        normalise(3)
+        cb_w, cb_s = pick_stationary("cb")
+        for h in range(2):
+            weave(nc.vector.tensor_copy, wb_woven[h], wb_raw[h][:])
+        for h in range(2):
+            quantise(wb_w[:, HALF * h : HALF * (h + 1)], wb_s[:, HALF * h : HALF * (h + 1)], wb_woven[h])
+        for t in range(PACK):
+            project(t)
+        cand_w, cand_s = pick_stationary("cand")
+        scores(0)
+        scores(1)
+
+        gb = [sq[c // 2][:, S * (c % 2) : S * (c % 2 + 1)] for c in range(4)]
+        root_t = [sb("root_t%d" % c, [P, S], F32) for c in range(4)]
+        inv_t = [sb("inv_t%d" % c, [P, S], F32) for c in range(4)]
+        res_s = sb("res_s", [P, S], U8)
+        out_rows = out_0.rearrange("(p t) j -> p t j", t=PACK)
+        out_words = out_1[0].rearrange("p c r -> p (c r)").bitcast(I32)
+
+        def fetch_b(c):
+            for t in range(PACK):
+                nc.scalar.activation(out=gb[c][:, block(t)], in_=ab[:, t, :].indirect(entries("n4", BLK * c, BLK)), func=ACT.Copy)
+
+        def denominator(c):
+            for t in range(PACK):
+                transpose_sum(bank[c][:, block(t)], ab[:, t, block(c)], gb[c][:, block(t)])
+            nc.scalar.activation(out=root_t[c][:], in_=bank[c][:], func=ACT.Abs_reciprocal_sqrt, bias=0.5)
+            nc.vector.tensor_tensor(out=inv_t[c][:], in0=root_t[c][:], in1=root_t[c][:], op=ALU.mult)
+            for t in range(PACK):
+                nc.tensor.transpose(bank[c][:, block(t)], inv_t[c][:, block(t)], ident[:])
+
+        def result(first, width):
+            c, lo = divmod(first, BLK)
+            ga = sb("ga%d" % first, [P, PACK, width], F32)
+            diff = sb("diff%d" % first, [P, PACK, width], F32)
+            res = sb("res%d" % first, [P, PACK, width], F32)
+            res_woven = sb("res_woven%d" % first, [P, width, PACK], BF16)
+            res_w = sb("res_w%d" % first, [P, width], U32)
+            cols = slice(first, first + width)
+            for t in range(PACK):
+                nc.scalar.activation(out=ga[:, t, :], in_=aw[:, t, :].indirect(entries("n3", first, width)), func=ACT.Copy)
+            nc.vector.scalar_tensor_tensor(
+                out=diff[:], in0=a_bank[c][:].rearrange("p (t j) -> p t j", t=PACK)[:, :, lo : lo + width], scalar=0.0625,
+                in1=ga[:], op0=ALU.mult, op1=ALU.subtract,
+            )
+            nc.vector.tensor_tensor(
+                out=res[:], in0=bank[c][:].rearrange("p (t j) -> p t j", t=PACK)[:, :, lo : lo + width], in1=diff[:], op=ALU.mult
+            )
+            nc.sync.dma_start(out_rows[:, :, cols], res[:])
+            weave(nc.vector.tensor_copy, res_woven, res[:])
+            quantise(res_w[:], res_s[:, cols], res_woven)
+            nc.sync.dma_start(out_words[:, cols], res_w[:].bitcast(I32))
+
+        fetch_b(0)
+        fetch_b(1)
+        denominator(0)
+        fetch_b(2)
+        denominator(1)
+        result(0, 128)
+        fetch_b(3)
+        denominator(2)
+        result(128, 128)
+        denominator(3)
+        result(256, 128)
+        result(384, 64)
+        result(448, 64)
+        for q in range(4):
+            (nc.sync, nc.scalar)[q % 2].dma_start(out_2[0, 4 * q : 4 * q + 4, :].bitcast(I32), res_s[32 * q : 32 * q + 4, :].bitcast(I32))

@@ -46,9 +46,9 @@ def tile_picked_cdswnormbstd_none_po_kernel(
         def entries(name, first, count):
             return lists[name][:, first // 16 : (first + count) // 16]
 
-        def load_scale_rows(dst, src, queues):
-            for q in range(4):
-                queues[q].dma_start(dst[32 * q : 32 * q + 4, :].bitcast(I32), src[0, 4 * q : 4 * q + 4, :].bitcast(I32))
+        def load_scale_rows(dst, src, quadrants):
+            for q in quadrants:
+                nc.sync.dma_start(dst[32 * q : 32 * q + 4, :].bitcast(I32), src[0, 4 * q : 4 * q + 4, :].bitcast(I32))
 
         def weave(engine_copy, dst, planes):
             engine_copy(
@@ -74,22 +74,27 @@ def tile_picked_cdswnormbstd_none_po_kernel(
         nc.gpsimd.memset(w1s_raw[:].bitcast(I32), 0)
         load_list("offs", offs)
         nc.sync.dma_start(w1w_raw[:].bitcast(I32), w1_words[0].bitcast(I32))
-        load_scale_rows(xs, x_scales, [nc.sync] * 4)
+        load_scale_rows(w1s_raw, w1_scales, range(1))
+        load_scale_rows(xs, x_scales, range(4))
         nc.sync.dma_start(xw[:].bitcast(I32), x_words[0].rearrange("p c r -> p (c r)").bitcast(I32))
-        load_scale_rows(w1s_raw, w1_scales, [nc.gpsimd, nc.gpsimd, nc.sync, nc.sync])
+        load_scale_rows(w1s_raw, w1_scales, range(1, 4))
         load_list("n1", n1)
         load_list("n2", n2)
+        load_list("cb", cb)
+        gain = sb("gain", [P, PACK], F32)
+        nc.sync.dma_start(gain[:], gs.rearrange("(p t) o -> p (t o)", t=PACK))
         wb_raw = [sb("wb_raw%d" % h, [P, PACK, HALF], F32) for h in range(2)]
         wb_rows = wb.rearrange("(p t) j -> p t j", t=PACK)
         nc.sync.dma_start(wb_raw[0][:], wb_rows[:, :, 0:HALF])
         nc.sync.dma_start(wb_raw[1][:], wb_rows[:, :, HALF:S])
-        gain = sb("gain", [P, PACK], F32)
-        nc.sync.dma_start(gain[:], gs.rearrange("(p t) o -> p (t o)", t=PACK))
-        load_list("cb", cb)
         load_list("cand", cand)
         load_list("n4", n4)
         load_list("n3", n3)
 
+
+        warm = sb("warm", [P, 2], F32)
+        nc.gpsimd.memset(warm[:, 0:1], 1.0)
+        nc.scalar.activation(out=warm[:, 1:2], in_=warm[:, 0:1], func=ACT.Abs_reciprocal_sqrt)
 
         w1w = sb("w1w", [P, 2 * S], U8)
         w1s = sb("w1s", [P, S], U8)
@@ -155,12 +160,12 @@ def tile_picked_cdswnormbstd_none_po_kernel(
         sq = [sb("sq%d" % i, [P, 2 * S], F32) for i in range(2)]
         rs = [sb("rs%d" % i, [P, 2, HALF], F32) for i in range(2)]
         d0 = [sb("d0%d" % i, [P, 2, HALF], F32) for i in range(2)]
-        z_planes = [sb("z_planes%d" % h, [P, PACK, HALF], F32) for h in range(2)]
         z_woven = [sb("z_woven%d" % h, [P, HALF, PACK], BF16) for h in range(2)]
         z_w = [sb("z_w%d" % h, [P, HALF], U32) for h in range(2)]
         z_s = [sb("z_s%d" % h, [P, HALF], U8) for h in range(2)]
         a_bank = [bank[6], bank[7], bank[4], bank[5]]
         aw = sb("aw", [P, PACK, S], F32)
+        z_planes = [aw[:, :, HALF:S], aw[:, :, 0:HALF]]
 
         def fetch(u):
             h, pair = divmod(u, 2)
@@ -172,12 +177,13 @@ def tile_picked_cdswnormbstd_none_po_kernel(
         def sums(u):
             h, pair = divmod(u, 2)
             nc.vector.tensor_tensor(out=us[pair][:], in0=pa[pair][:], in1=nb[pair][:], op=ALU.subtract)
-            for k in range(4):
-                i, jb = divmod(k, 2)
-                transpose_sum(bank[2 * pair][:, block(k)], pa[pair][:, i, block(jb)], nb[pair][:, i, block(jb)])
-            for k in range(4):
-                i, jb = divmod(k, 2)
-                transpose_sum(bank[2 * pair + 1][:, block(k)], yw[2 * pair + i][:, block(2 * h + jb)], us[pair][:, i, block(jb)])
+            for kind in ((1, 0) if h == 0 else (0, 1)):
+                for k in range(4):
+                    i, jb = divmod(k, 2)
+                    if kind == 1:
+                        transpose_sum(bank[2 * pair + 1][:, block(k)], yw[2 * pair + i][:, block(2 * h + jb)], us[pair][:, i, block(jb)])
+                    else:
+                        transpose_sum(bank[2 * pair][:, block(k)], pa[pair][:, i, block(jb)], nb[pair][:, i, block(jb)])
             for i in range(2):
                 nc.vector.scalar_tensor_tensor(
                     out=d0[pair][:, i, :], in0=yw[2 * pair + i][:, HALF * h : HALF * (h + 1)], scalar=-1.32,
@@ -186,8 +192,11 @@ def tile_picked_cdswnormbstd_none_po_kernel(
 
         def squares(u):
             pair = u % 2
-            nc.scalar.activation(out=sq[pair][:, 0:S], in_=bank[2 * pair][:], func=ACT.Square, scale=3.2)
             nc.scalar.activation(out=sq[pair][:, S : 2 * S], in_=bank[2 * pair + 1][:], func=ACT.Square, scale=1.2)
+            nc.scalar.activation(out=sq[pair][:, 0:S], in_=bank[2 * pair][:], func=ACT.Square, scale=3.2)
+
+        def add_squares(u):
+            pair = u % 2
             for k in range(4):
                 transpose_sum(bank[4 + pair][:, block(k)], sq[pair][:, block(k)], sq[pair][:, block(4 + k)])
 
@@ -204,9 +213,11 @@ def tile_picked_cdswnormbstd_none_po_kernel(
                     in1=rs[pair][:, i, :], op0=ALU.mult, op1=ALU.mult,
                 )
 
-        def scores(h):
-            weave(nc.vector.tensor_copy, z_woven[h], z_planes[h][:])
+        def quantise_z(h):
+            weave(nc.vector.tensor_copy, z_woven[h], z_planes[h])
             quantise(z_w[h][:], z_s[h][:], z_woven[h])
+
+        def scores(h):
             for c in range(2):
                 for t in range(PACK):
                     nc.tensor.matmul_mx(
@@ -229,10 +240,10 @@ def tile_picked_cdswnormbstd_none_po_kernel(
 
         def project(t):
             nc.tensor.matmul_mx(
-                out=bank[6 + t % 2][:], lhsT=cb_w[:, block(t)].bitcast(FP8X4), lhsT_scale=cb_s[:, block(t)],
+                out=bank[t][:], lhsT=cb_w[:, block(t)].bitcast(FP8X4), lhsT_scale=cb_s[:, block(t)],
                 rhs=wb_w[:].bitcast(FP8X4), rhs_scale=wb_s[:], start=True, stop=True,
             )
-            nc.scalar.activation(out=ab[:, t, :], in_=bank[6 + t % 2][:], func=ACT.Abs)
+            nc.scalar.activation(out=ab[:, t, :], in_=bank[t][:], func=ACT.Abs)
 
         fetch(0)
         fetch(1)
@@ -240,16 +251,22 @@ def tile_picked_cdswnormbstd_none_po_kernel(
         squares(0)
         fetch(2)
         sums(1)
+        add_squares(0)
         normalise(0)
         squares(1)
         fetch(3)
         sums(2)
+        add_squares(1)
         normalise(1)
-        sums(3)
         squares(2)
+        sums(3)
+        add_squares(2)
         squares(3)
         normalise(2)
+        add_squares(3)
         normalise(3)
+        quantise_z(0)
+        quantise_z(1)
         cb_w, cb_s = pick_stationary("cb")
         for h in range(2):
             weave(nc.vector.tensor_copy, wb_woven[h], wb_raw[h][:])
@@ -261,9 +278,13 @@ def tile_picked_cdswnormbstd_none_po_kernel(
         scores(0)
         scores(1)
 
-        gb = [sq[c // 2][:, S * (c % 2) : S * (c % 2 + 1)] for c in range(4)]
         root_t = [sb("root_t%d" % c, [P, S], F32) for c in range(4)]
+        diff_all = sb("diff", [P, S], F32)
         inv_t = [sb("inv_t%d" % c, [P, S], F32) for c in range(4)]
+        gb = [sq[0][:, 0:S], sq[1][:, 0:S], inv_t[0][:], inv_t[1][:]]
+        ga_rows = [gb[1], gb[2], gb[3], inv_t[2][:]]
+        res_rows = [sb("res%d" % c, [P, PACK, BLK], F32) for c in range(4)]
+        res_w = [sb("res_w%d" % h, [P, HALF], U32) for h in range(2)]
         res_s = sb("res_s", [P, S], U8)
         out_rows = out_0.rearrange("(p t) j -> p t j", t=PACK)
         out_words = out_1[0].rearrange("p c r -> p (c r)").bitcast(I32)
@@ -275,18 +296,21 @@ def tile_picked_cdswnormbstd_none_po_kernel(
         def denominator(c):
             for t in range(PACK):
                 transpose_sum(bank[c][:, block(t)], ab[:, t, block(c)], gb[c][:, block(t)])
+
+        def invert(c):
             nc.scalar.activation(out=root_t[c][:], in_=bank[c][:], func=ACT.Abs_reciprocal_sqrt, bias=0.5)
             nc.vector.tensor_tensor(out=inv_t[c][:], in0=root_t[c][:], in1=root_t[c][:], op=ALU.mult)
+
+        def turn_back(c):
             for t in range(PACK):
                 nc.tensor.transpose(bank[c][:, block(t)], inv_t[c][:, block(t)], ident[:])
 
-        def result(first, width):
+        def result(first, width, copy):
             c, lo = divmod(first, BLK)
-            ga = sb("ga%d" % first, [P, PACK, width], F32)
-            diff = sb("diff%d" % first, [P, PACK, width], F32)
-            res = sb("res%d" % first, [P, PACK, width], F32)
+            ga = ga_rows[c][:, PACK * lo : PACK * (lo + width)].rearrange("p (t j) -> p t j", t=PACK)
+            diff = diff_all[:, PACK * lo : PACK * (lo + width)].rearrange("p (t j) -> p t j", t=PACK)
+            res = res_rows[c][:, :, lo : lo + width]
             res_woven = sb("res_woven%d" % first, [P, width, PACK], BF16)
-            res_w = sb("res_w%d" % first, [P, width], U32)
             cols = slice(first, first + width)
             for t in range(PACK):
                 nc.scalar.activation(out=ga[:, t, :], in_=aw[:, t, :].indirect(entries("n3", first, width)), func=ACT.Copy)
@@ -295,25 +319,36 @@ def tile_picked_cdswnormbstd_none_po_kernel(
                 in1=ga[:], op0=ALU.mult, op1=ALU.subtract,
             )
             nc.vector.tensor_tensor(
-                out=res[:], in0=bank[c][:].rearrange("p (t j) -> p t j", t=PACK)[:, :, lo : lo + width], in1=diff[:], op=ALU.mult
+                out=res, in0=bank[c][:].rearrange("p (t j) -> p t j", t=PACK)[:, :, lo : lo + width], in1=diff[:], op=ALU.mult
             )
-            nc.sync.dma_start(out_rows[:, :, cols], res[:])
-            weave(nc.vector.tensor_copy, res_woven, res[:])
-            quantise(res_w[:], res_s[:, cols], res_woven)
-            nc.sync.dma_start(out_words[:, cols], res_w[:].bitcast(I32))
+            if lo + width == BLK:
+                nc.sync.dma_start(out_rows[:, :, block(c)], res_rows[c][:])
+            weave(copy, res_woven, res)
+            h, place = divmod(first, HALF)
+            quantise(res_w[h][:, place : place + width], res_s[:, cols], res_woven)
+            if place + width == HALF:
+                nc.sync.dma_start(out_words[:, HALF * h : HALF * (h + 1)], res_w[h][:].bitcast(I32))
 
         fetch_b(0)
         fetch_b(1)
         denominator(0)
-        fetch_b(2)
+        invert(0)
         denominator(1)
-        result(0, 128)
-        fetch_b(3)
+        turn_back(0)
+        result(0, 128, nc.vector.tensor_copy)
+        invert(1)
+        fetch_b(2)
         denominator(2)
-        result(128, 128)
+        turn_back(1)
+        result(128, 128, nc.vector.tensor_copy)
+        invert(2)
+        fetch_b(3)
         denominator(3)
-        result(256, 128)
-        result(384, 64)
-        result(448, 64)
+        invert(3)
+        turn_back(2)
+        result(256, 128, nc.scalar.copy)
+        turn_back(3)
+        result(384, 64, nc.scalar.copy)
+        result(448, 64, nc.vector.tensor_copy)
         for q in range(4):
             (nc.sync, nc.scalar)[q % 2].dma_start(out_2[0, 4 * q : 4 * q + 4, :].bitcast(I32), res_s[32 * q : 32 * q + 4, :].bitcast(I32))

@@ -32,8 +32,8 @@ def tile_picked_cdswnormbstd_none_po_kernel(
         keep = ctx.enter_context(tc.tile_pool(name="keep", bufs=1))
         psum = ctx.enter_context(tc.psum_pool(name="psum", bufs=1))
 
-        def sb(name, shape, dtype):
-            return keep.tile(shape, dtype, name=name, align_bytes=64)
+        def sb(name, shape, dtype, tag=None):
+            return keep.tile(shape, dtype, name=name, tag=tag or name, align_bytes=64)
 
         bank = [psum.tile([P, S], F32, name="bank%d" % i) for i in range(8)]
 
@@ -116,11 +116,14 @@ def tile_picked_cdswnormbstd_none_po_kernel(
             nc.vector.tensor_copy(out=xq_s[h][:], in_=xs[:].indirect(entries("offs", HALF * h, HALF)))
             nc.vector.tensor_copy(out=xq_w[h][:], in_=xw[:].indirect(entries("offs", HALF * h, HALF)))
 
-        for pair in range(2):
+        def y_part(t, h):
+            return bank[4 + t % 2 if t >= 2 or h == 0 else t][:, HALF * h : HALF * (h + 1)]
+
+        def project_y(pair):
             for h in range(2):
                 for t in (2 * pair, 2 * pair + 1):
                     nc.tensor.matmul_mx(
-                        out=bank[t][:, HALF * h : HALF * (h + 1)],
+                        out=y_part(t, h),
                         lhsT=w1w[:, 2 * BLK * t : 2 * BLK * (t + 1)].bitcast(FP4X4),
                         lhsT_scale=w1s[:, block(t)],
                         rhs=xq_w[h][:].bitcast(FP8X4),
@@ -129,6 +132,7 @@ def tile_picked_cdswnormbstd_none_po_kernel(
                         stop=True,
                     )
 
+        project_y(0)
         ident = sb("ident", [P, P], F32)
         make_identity(nc, ident[:])
 
@@ -136,9 +140,12 @@ def tile_picked_cdswnormbstd_none_po_kernel(
 
         Y_SCALE = -25.0 / 48.0
         yw = [sb("yw%d" % t, [P, S], F32) for t in range(PACK)]
-        nc.scalar.activation(out=yw[0][:], in_=bank[0][:], func=ACT.Copy, scale=Y_SCALE)
-        for t in range(1, PACK):
-            nc.vector.tensor_scalar(out=yw[t][:], in0=bank[t][:], scalar1=Y_SCALE, scalar2=None, op0=ALU.mult)
+        for h in range(2):
+            for t in range(2):
+                nc.scalar.activation(out=yw[t][:, HALF * h : HALF * (h + 1)], in_=y_part(t, h), func=ACT.Copy, scale=Y_SCALE)
+        project_y(1)
+        for t in range(2, PACK):
+            nc.vector.tensor_scalar(out=yw[t][:], in0=bank[4 + t % 2][:], scalar1=Y_SCALE, scalar2=None, op0=ALU.mult)
 
         def pick_stationary(name):
             words = sb(name + "_gw", [P, S], U32)
@@ -154,13 +161,15 @@ def tile_picked_cdswnormbstd_none_po_kernel(
             deal_bytes(nc.vector, dealt_s, scales)
             return dealt_w, dealt_s
 
-        pa = [sb("pa%d" % i, [P, 2, HALF], F32) for i in range(2)]
-        nb = [sb("nb%d" % i, [P, 2, HALF], F32) for i in range(2)]
+        ab = sb("ab", [P, PACK, S], F32)
+        pa = [ab[:, 2 - 2 * i, :].rearrange("p (i j) -> p i j", i=2) for i in range(2)]
+        nb = [ab[:, 3 - 2 * i, :].rearrange("p (i j) -> p i j", i=2) for i in range(2)]
         us = [sb("us%d" % i, [P, 2, HALF], F32) for i in range(2)]
         sq = [sb("sq%d" % i, [P, 2 * S], F32) for i in range(2)]
-        rs = [sb("rs%d" % i, [P, 2, HALF], F32) for i in range(2)]
-        d0 = [sb("d0%d" % i, [P, 2, HALF], F32) for i in range(2)]
-        z_woven = [sb("z_woven%d" % h, [P, HALF, PACK], BF16) for h in range(2)]
+        factors = [sb("factors%d" % i, [P, 4, HALF], F32) for i in range(2)]
+        rs = [factors[i][:, 0:2, :] for i in range(2)]
+        d0 = [factors[i][:, 2:4, :] for i in range(2)]
+        z_woven = [sb("z_woven%d" % c, [P, BLK, PACK], BF16) for c in range(4)]
         z_w = [sb("z_w%d" % h, [P, HALF], U32) for h in range(2)]
         z_s = [sb("z_s%d" % h, [P, HALF], U8) for h in range(2)]
         a_bank = [bank[6], bank[7], bank[4], bank[5]]
@@ -176,7 +185,7 @@ def tile_picked_cdswnormbstd_none_po_kernel(
 
         def sums(u):
             h, pair = divmod(u, 2)
-            nc.vector.tensor_tensor(out=us[pair][:], in0=pa[pair][:], in1=nb[pair][:], op=ALU.subtract)
+            nc.vector.tensor_tensor(out=us[pair][:], in0=pa[pair], in1=nb[pair], op=ALU.subtract)
             for kind in ((1, 0) if h == 0 else (0, 1)):
                 for k in range(4):
                     i, jb = divmod(k, 2)
@@ -203,7 +212,7 @@ def tile_picked_cdswnormbstd_none_po_kernel(
         def normalise(u):
             h, pair = divmod(u, 2)
             nc.scalar.activation(
-                out=rs[pair][:].rearrange("p i j -> p (i j)"), in_=bank[4 + pair][:],
+                out=rs[pair].rearrange("p i j -> p (i j)"), in_=bank[4 + pair][:],
                 func=ACT.Abs_reciprocal_sqrt, scale=0.5, bias=0.25,
             )
             for i in range(2):
@@ -214,8 +223,10 @@ def tile_picked_cdswnormbstd_none_po_kernel(
                 )
 
         def quantise_z(h):
-            weave(nc.vector.tensor_copy, z_woven[h], z_planes[h])
-            quantise(z_w[h][:], z_s[h][:], z_woven[h])
+            for c in range(2):
+                weave(nc.vector.tensor_copy, z_woven[2 * h + c], z_planes[h][:, :, block(c)])
+            for c in range(2):
+                quantise(z_w[h][:, block(c)], z_s[h][:, block(c)], z_woven[2 * h + c])
 
         def scores(h):
             for c in range(2):
@@ -236,70 +247,52 @@ def tile_picked_cdswnormbstd_none_po_kernel(
 
         wb_w = sb("wb_w", [P, S], U32)
         wb_s = sb("wb_s", [P, S], U8)
-        ab = sb("ab", [P, PACK, S], F32)
+        b_bank = [bank[6], bank[7], bank[0], bank[1]]
 
         def project(t):
             nc.tensor.matmul_mx(
-                out=bank[t][:], lhsT=cb_w[:, block(t)].bitcast(FP8X4), lhsT_scale=cb_s[:, block(t)],
+                out=b_bank[t][:], lhsT=cb_w[:, block(t)].bitcast(FP8X4), lhsT_scale=cb_s[:, block(t)],
                 rhs=wb_w[:].bitcast(FP8X4), rhs_scale=wb_s[:], start=True, stop=True,
             )
-            nc.scalar.activation(out=ab[:, t, :], in_=bank[t][:], func=ACT.Abs)
 
-        fetch(0)
-        fetch(1)
-        sums(0)
-        squares(0)
-        fetch(2)
-        sums(1)
-        add_squares(0)
-        normalise(0)
-        squares(1)
-        fetch(3)
-        sums(2)
-        add_squares(1)
-        normalise(1)
-        squares(2)
-        sums(3)
-        add_squares(2)
-        squares(3)
-        normalise(2)
-        add_squares(3)
-        normalise(3)
-        quantise_z(0)
-        quantise_z(1)
-        cb_w, cb_s = pick_stationary("cb")
-        for h in range(2):
-            weave(nc.vector.tensor_copy, wb_woven[h], wb_raw[h][:])
-        for h in range(2):
-            quantise(wb_w[:, HALF * h : HALF * (h + 1)], wb_s[:, HALF * h : HALF * (h + 1)], wb_woven[h])
-        for t in range(PACK):
-            project(t)
-        cand_w, cand_s = pick_stationary("cand")
-        scores(0)
-        scores(1)
+        def size(t):
+            if t in (1,):
+                plain = sb("b_plain%d" % t, [P, S], F32)
+                nc.vector.tensor_copy(out=plain[:], in_=b_bank[t][:])
+                nc.vector.scalar_tensor_tensor(out=ab[:, t, :], in0=b_bank[t][:], scalar=-1.0, in1=plain[:], op0=ALU.mult, op1=ALU.max)
+            else:
+                nc.scalar.activation(out=ab[:, t, :], in_=b_bank[t][:], func=ACT.Abs)
 
-        root_t = [sb("root_t%d" % c, [P, S], F32) for c in range(4)]
-        diff_all = sb("diff", [P, S], F32)
+        root_pairs = []
+        diff_all = [sb("diff%d" % i, [P, S], F32) for i in range(2)]
         inv_t = [sb("inv_t%d" % c, [P, S], F32) for c in range(4)]
-        gb = [sq[0][:, 0:S], sq[1][:, 0:S], inv_t[0][:], inv_t[1][:]]
-        ga_rows = [gb[1], gb[2], gb[3], inv_t[2][:]]
+        flat = "p i j -> p (i j)"
+        gb_half = [sq[0][:].rearrange("p (t j) -> p t j", t=PACK), factors[1][:]]
+        gb = [gb_half[c // 2][:, :, block(c % 2)] for c in range(4)]
+        ga_rows = [gb[1], gb[2], gb[3], inv_t[2][:].rearrange("p (t j) -> p t j", t=PACK)]
         res_rows = [sb("res%d" % c, [P, PACK, BLK], F32) for c in range(4)]
         res_w = [sb("res_w%d" % h, [P, HALF], U32) for h in range(2)]
         res_s = sb("res_s", [P, S], U8)
         out_rows = out_0.rearrange("(p t) j -> p t j", t=PACK)
         out_words = out_1[0].rearrange("p c r -> p (c r)").bitcast(I32)
 
-        def fetch_b(c):
+        def fetch_b(h):
             for t in range(PACK):
-                nc.scalar.activation(out=gb[c][:, block(t)], in_=ab[:, t, :].indirect(entries("n4", BLK * c, BLK)), func=ACT.Copy)
+                nc.scalar.activation(out=gb_half[h][:, t, :], in_=ab[:, t, :].indirect(entries("n4", HALF * h, HALF)), func=ACT.Copy)
 
         def denominator(c):
             for t in range(PACK):
-                transpose_sum(bank[c][:, block(t)], ab[:, t, block(c)], gb[c][:, block(t)])
+                transpose_sum(bank[c][:, block(t)], ab[:, t, block(c)], gb[c][:, t, :])
 
         def invert(c):
-            nc.scalar.activation(out=root_t[c][:], in_=bank[c][:], func=ACT.Abs_reciprocal_sqrt, bias=0.5)
-            nc.vector.tensor_tensor(out=inv_t[c][:], in0=root_t[c][:], in1=root_t[c][:], op=ALU.mult)
+            if c % 2 == 0:
+                root_pairs.append(sb("roots%d" % c, [P, 2, S], F32, tag=("cand_w", "cand_s")[c // 2]))
+            root = root_pairs[c // 2][:, c % 2, :]
+            nc.scalar.activation(out=root, in_=bank[c][:], func=ACT.Abs_reciprocal_sqrt, bias=0.5)
+            if c in (3,):
+                nc.scalar.activation(out=inv_t[c][:], in_=root, func=ACT.Square)
+            else:
+                nc.vector.tensor_tensor(out=inv_t[c][:], in0=root, in1=root, op=ALU.mult)
 
         def turn_back(c):
             for t in range(PACK):
@@ -307,8 +300,8 @@ def tile_picked_cdswnormbstd_none_po_kernel(
 
         def result(first, width, copy):
             c, lo = divmod(first, BLK)
-            ga = ga_rows[c][:, PACK * lo : PACK * (lo + width)].rearrange("p (t j) -> p t j", t=PACK)
-            diff = diff_all[:, PACK * lo : PACK * (lo + width)].rearrange("p (t j) -> p t j", t=PACK)
+            ga = ga_rows[c][:, :, lo : lo + width]
+            diff = diff_all[c % 2][:, PACK * lo : PACK * (lo + width)].rearrange("p (t j) -> p t j", t=PACK)
             res = res_rows[c][:, :, lo : lo + width]
             res_woven = sb("res_woven%d" % first, [P, width, PACK], BF16)
             cols = slice(first, first + width)
@@ -323,27 +316,65 @@ def tile_picked_cdswnormbstd_none_po_kernel(
             )
             if lo + width == BLK:
                 nc.sync.dma_start(out_rows[:, :, block(c)], res_rows[c][:])
-            weave(copy, res_woven, res)
+            if copy is None:
+                nc.gpsimd.tensor_copy(out=res_woven[:], in_=res.rearrange("p t j -> p j t"))
+            else:
+                weave(copy, res_woven, res)
             h, place = divmod(first, HALF)
             quantise(res_w[h][:, place : place + width], res_s[:, cols], res_woven)
             if place + width == HALF:
                 nc.sync.dma_start(out_words[:, HALF * h : HALF * (h + 1)], res_w[h][:].bitcast(I32))
 
+        fetch(0)
+        fetch(1)
+        sums(0)
+        squares(0)
+        fetch(2)
+        sums(1)
+        add_squares(0)
+        cb_w, cb_s = pick_stationary("cb")
+        for h in range(2):
+            weave(nc.vector.tensor_copy, wb_woven[h], wb_raw[h][:])
+        for h in range(2):
+            quantise(wb_w[:, HALF * h : HALF * (h + 1)], wb_s[:, HALF * h : HALF * (h + 1)], wb_woven[h])
+        project(0)
+        project(1)
+        normalise(0)
+        squares(1)
+        fetch(3)
+        sums(2)
+        add_squares(1)
+        normalise(1)
+        squares(2)
+        sums(3)
+        size(0)
+        size(1)
+        add_squares(2)
+        squares(3)
+        normalise(2)
+        add_squares(3)
+        normalise(3)
+        quantise_z(0)
+        quantise_z(1)
+        for t in (2, 3):
+            project(t)
+            size(t)
+        cand_w, cand_s = pick_stationary("cand")
+        scores(0)
         fetch_b(0)
-        fetch_b(1)
         denominator(0)
+        scores(1)
         invert(0)
         denominator(1)
+        fetch_b(1)
         turn_back(0)
-        result(0, 128, nc.vector.tensor_copy)
         invert(1)
-        fetch_b(2)
         denominator(2)
+        result(0, 128, nc.vector.tensor_copy)
         turn_back(1)
-        result(128, 128, nc.vector.tensor_copy)
         invert(2)
-        fetch_b(3)
         denominator(3)
+        result(128, 128, nc.vector.tensor_copy)
         invert(3)
         turn_back(2)
         result(256, 128, nc.scalar.copy)

@@ -269,7 +269,8 @@ def tile_picked_cdswnormbstd_none_po_kernel(
         flat = "p i j -> p (i j)"
         gb_half = [sq[0][:].rearrange("p (t j) -> p t j", t=PACK), factors[1][:]]
         gb = [gb_half[c // 2][:, :, block(c % 2)] for c in range(4)]
-        ga_rows = [gb[1], gb[2], gb[3], inv_t[2][:].rearrange("p (t j) -> p t j", t=PACK)]
+        planes = [inv_t[c][:].rearrange("p (t j) -> p t j", t=PACK) for c in range(4)]
+        ga_rows = [gb[1], gb[2], planes[1], planes[2]]
         res_rows = [sb("res%d" % c, [P, PACK, BLK], F32) for c in range(4)]
         res_w = [sb("res_w%d" % h, [P, HALF], U32) for h in range(2)]
         res_s = sb("res_s", [P, S], U8)
@@ -289,7 +290,7 @@ def tile_picked_cdswnormbstd_none_po_kernel(
                 root_pairs.append(sb("roots%d" % c, [P, 2, S], F32, tag=("cand_w", "cand_s")[c // 2]))
             root = root_pairs[c // 2][:, c % 2, :]
             nc.scalar.activation(out=root, in_=bank[c][:], func=ACT.Abs_reciprocal_sqrt, bias=0.5)
-            if c in (3,):
+            if c in ():
                 nc.scalar.activation(out=inv_t[c][:], in_=root, func=ACT.Square)
             else:
                 nc.vector.tensor_tensor(out=inv_t[c][:], in0=root, in1=root, op=ALU.mult)
@@ -367,15 +368,15 @@ def tile_picked_cdswnormbstd_none_po_kernel(
         invert(0)
         denominator(1)
         fetch_b(1)
-        turn_back(0)
         invert(1)
         denominator(2)
+        turn_back(0)
         result(0, 128, nc.vector.tensor_copy)
-        turn_back(1)
         invert(2)
         denominator(3)
-        result(128, 128, nc.vector.tensor_copy)
         invert(3)
+        turn_back(1)
+        result(128, 128, nc.vector.tensor_copy)
         turn_back(2)
         result(256, 128, nc.scalar.copy)
         turn_back(3)

from contextlib import ExitStack

import concourse.mybir as mybir
from concourse.masks import make_identity

F32 = mybir.dt.float32
BF16 = mybir.dt.bfloat16
I32 = mybir.dt.int32
U32 = mybir.dt.uint32
U16 = mybir.dt.uint16
U8 = mybir.dt.uint8
FP8X4 = mybir.dt.float8_e4m3fn_x4
FP4X4 = mybir.dt.float4_e2m1fn_x4
ACT = mybir.ActivationFunctionType
ALU = mybir.AluOpType

P = 128
PACK = 4
TOKENS = 2048
S = 512
HALF = 256
BLK = 128
LIST_COLS = S // 16
FLOPS = 3 * 2 * 512 * 512 * 512


def tile_picked_cdswnormbstd_none_po_kernel(
    tc, x_words, x_scales, w1_words, w1_scales, gs, wb, offs, n1, n2, cand, cb, n3, n4, out_0, out_1, out_2
):
    nc = tc.nc
    with ExitStack() as ctx:
        keep = ctx.enter_context(tc.tile_pool(name="keep", bufs=1))
        psum = ctx.enter_context(tc.psum_pool(name="psum", bufs=1))

        def sb(name, shape, dtype, tag=None):
            return keep.tile(shape, dtype, name=name, tag=tag or name, align_bytes=64)

        bank = [psum.tile([P, S], F32, name="bank%d" % i) for i in range(8)]

        lists = {}

        def load_list(name, src):
            lists[name] = sb("list_" + name, [P, LIST_COLS], U16)
            nc.sync.dma_start(lists[name][:], src)

        def entries(name, first, count):
            return lists[name][:, first // 16 : (first + count) // 16]

        def load_scale_rows(dst, src, quadrants):
            for q in quadrants:
                nc.sync.dma_start(dst[32 * q : 32 * q + 4, :].bitcast(I32), src[0, 4 * q : 4 * q + 4, :].bitcast(I32))

        def weave(engine_copy, dst, planes):
            engine_copy(
                out=dst[:].rearrange("p (c i) t -> p c t i", i=4),
                in_=planes.rearrange("p t (c i) -> p c t i", i=4),
            )

        def quantise(codes, scales, woven):
            nc.vector.quantize_mx(out=codes.bitcast(FP8X4), scales=scales, in_=woven[:].rearrange("p j t -> p (j t)"))

        def transpose_sum(dst, first, second):
            nc.tensor.matmul(dst, lhsT=first, rhs=ident[:], is_transpose=True, start=True, stop=False)
            nc.tensor.matmul(dst, lhsT=second, rhs=ident[:], is_transpose=True, start=False, stop=True)

        def block(k):
            return slice(BLK * k, BLK * (k + 1))

        xs = sb("xs", [P, TOKENS], U8)
        xw = sb("xw", [P, TOKENS], U32)
        w1w_raw = sb("w1w_raw", [P, 2 * S], U8)
        w1s_raw = sb("w1s_raw", [P, S], U8)
        nc.vector.memset(xs[:].bitcast(I32), 0)
        nc.gpsimd.memset(w1s_raw[:].bitcast(I32), 0)
        load_list("offs", offs)
        nc.sync.dma_start(w1w_raw[:].bitcast(I32), w1_words[0].bitcast(I32))
        load_scale_rows(w1s_raw, w1_scales, range(1))
        load_scale_rows(xs, x_scales, range(4))
        nc.sync.dma_start(xw[:].bitcast(I32), x_words[0].rearrange("p c r -> p (c r)").bitcast(I32))
        load_scale_rows(w1s_raw, w1_scales, range(1, 4))
        load_list("n1", n1)
        load_list("n2", n2)
        load_list("cb", cb)
        gain = sb("gain", [P, PACK], F32)
        nc.sync.dma_start(gain[:], gs.rearrange("(p t) o -> p (t o)", t=PACK))
        wb_raw = [sb("wb_raw%d" % h, [P, PACK, HALF], F32) for h in range(2)]
        wb_rows = wb.rearrange("(p t) j -> p t j", t=PACK)
        nc.sync.dma_start(wb_raw[0][:], wb_rows[:, :, 0:HALF])
        nc.sync.dma_start(wb_raw[1][:], wb_rows[:, :, HALF:S])
        load_list("cand", cand)
        load_list("n4", n4)
        load_list("n3", n3)


        warm = sb("warm", [P, 2], F32)
        nc.gpsimd.memset(warm[:, 0:1], 1.0)
        nc.scalar.activation(out=warm[:, 1:2], in_=warm[:, 0:1], func=ACT.Abs_reciprocal_sqrt)

        w1w = sb("w1w", [P, 2 * S], U8)
        w1s = sb("w1s", [P, S], U8)
        nc.vector.tensor_copy(
            out=w1w[:].rearrange("p (t c i b) -> p c t i b", t=PACK, i=8, b=2),
            in_=w1w_raw[:].rearrange("p (c i t b) -> p c t i b", t=PACK, i=8, b=2),
        )

        def deal_bytes(engine, dst, src):
            engine.tensor_copy(
                out=dst[:].rearrange("p (t c i) -> p c t i", t=PACK, i=16),
                in_=src[:].rearrange("p (c i t) -> p c t i", t=PACK, i=16),
            )

        deal_bytes(nc.gpsimd, w1s, w1s_raw)
        xq_s = [sb("xq_s%d" % h, [P, HALF], U8) for h in range(2)]
        xq_w = [sb("xq_w%d" % h, [P, HALF], U32) for h in range(2)]
        for h in range(2):
            nc.vector.tensor_copy(out=xq_s[h][:], in_=xs[:].indirect(entries("offs", HALF * h, HALF)))
            nc.vector.tensor_copy(out=xq_w[h][:], in_=xw[:].indirect(entries("offs", HALF * h, HALF)))

        def y_part(t, h):
            return bank[4 + t % 2 if t >= 2 or h == 0 else t][:, HALF * h : HALF * (h + 1)]

        def project_y(pair):
            for h in range(2):
                for t in (2 * pair, 2 * pair + 1):
                    nc.tensor.matmul_mx(
                        out=y_part(t, h),
                        lhsT=w1w[:, 2 * BLK * t : 2 * BLK * (t + 1)].bitcast(FP4X4),
                        lhsT_scale=w1s[:, block(t)],
                        rhs=xq_w[h][:].bitcast(FP8X4),
                        rhs_scale=xq_s[h][:],
                        start=True,
                        stop=True,
                    )

        project_y(0)
        ident = sb("ident", [P, P], F32)
        make_identity(nc, ident[:])

        wb_woven = [sb("wb_woven%d" % h, [P, HALF, PACK], BF16) for h in range(2)]

        Y_SCALE = -25.0 / 48.0
        yw = [sb("yw%d" % t, [P, S], F32) for t in range(PACK)]
        for h in range(2):
            for t in range(2):
                nc.scalar.activation(out=yw[t][:, HALF * h : HALF * (h + 1)], in_=y_part(t, h), func=ACT.Copy, scale=Y_SCALE)
        project_y(1)
        for t in range(2, PACK):
            nc.vector.tensor_scalar(out=yw[t][:], in0=bank[4 + t % 2][:], scalar1=Y_SCALE, scalar2=None, op0=ALU.mult)

        def pick_stationary(name):
            words = sb(name + "_gw", [P, S], U32)
            scales = sb(name + "_gs", [P, S], U8)
            nc.vector.tensor_copy(out=words[:], in_=xw[:].indirect(lists[name][:]))
            nc.vector.tensor_copy(out=scales[:], in_=xs[:].indirect(lists[name][:]))
            dealt_w = sb(name + "_w", [P, S], U32)
            dealt_s = sb(name + "_s", [P, S], U8)
            nc.vector.tensor_copy(
                out=dealt_w[:].bitcast(I32).rearrange("p (t c i) -> p c t i", t=PACK, i=4),
                in_=words[:].bitcast(I32).rearrange("p (c i t) -> p c t i", t=PACK, i=4),
            )
            deal_bytes(nc.vector, dealt_s, scales)
            return dealt_w, dealt_s

        ab = sb("ab", [P, PACK, S], F32)
        pa = [ab[:, 2 - 2 * i, :].rearrange("p (i j) -> p i j", i=2) for i in range(2)]
        nb = [ab[:, 3 - 2 * i, :].rearrange("p (i j) -> p i j", i=2) for i in range(2)]
        us = [sb("us%d" % i, [P, 2, HALF], F32) for i in range(2)]
        sq = [sb("sq%d" % i, [P, 2 * S], F32) for i in range(2)]
        factors = [sb("factors%d" % i, [P, 4, HALF], F32) for i in range(2)]
        rs = [factors[i][:, 0:2, :] for i in range(2)]
        d0 = [factors[i][:, 2:4, :] for i in range(2)]
        z_woven = [sb("z_woven%d" % c, [P, BLK, PACK], BF16) for c in range(4)]
        z_w = [sb("z_w%d" % h, [P, HALF], U32) for h in range(2)]
        z_s = [sb("z_s%d" % h, [P, HALF], U8) for h in range(2)]
        a_bank = [bank[6], bank[7], bank[4], bank[5]]
        aw = sb("aw", [P, PACK, S], F32)
        z_planes = [aw[:, :, HALF:S], aw[:, :, 0:HALF]]

        def fetch(u):
            h, pair = divmod(u, 2)
            for i in range(2):
                window = yw[2 * pair + i]
                nc.scalar.activation(out=pa[pair][:, i, :], in_=window[:].indirect(entries("n1", HALF * h, HALF)), func=ACT.Copy, scale=-0.6)
                nc.scalar.activation(out=nb[pair][:, i, :], in_=window[:].indirect(entries("n2", HALF * h, HALF)), func=ACT.Copy, scale=0.6)

        def sums(u):
            h, pair = divmod(u, 2)
            nc.vector.tensor_tensor(out=us[pair][:], in0=pa[pair], in1=nb[pair], op=ALU.subtract)
            for kind in ((1, 0) if h == 0 else (0, 1)):
                for k in range(4):
                    i, jb = divmod(k, 2)
                    if kind == 1:
                        transpose_sum(bank[2 * pair + 1][:, block(k)], yw[2 * pair + i][:, block(2 * h + jb)], us[pair][:, i, block(jb)])
                    else:
                        transpose_sum(bank[2 * pair][:, block(k)], pa[pair][:, i, block(jb)], nb[pair][:, i, block(jb)])
            for i in range(2):
                nc.vector.scalar_tensor_tensor(
                    out=d0[pair][:, i, :], in0=yw[2 * pair + i][:, HALF * h : HALF * (h + 1)], scalar=-1.32,
                    in1=us[pair][:, i, :], op0=ALU.mult, op1=ALU.subtract,
                )

        def squares(u):
            pair = u % 2
            nc.scalar.activation(out=sq[pair][:, S : 2 * S], in_=bank[2 * pair + 1][:], func=ACT.Square, scale=1.2)
            nc.scalar.activation(out=sq[pair][:, 0:S], in_=bank[2 * pair][:], func=ACT.Square, scale=3.2)

        def add_squares(u):
            pair = u % 2
            for k in range(4):
                transpose_sum(bank[4 + pair][:, block(k)], sq[pair][:, block(k)], sq[pair][:, block(4 + k)])

        def normalise(u):
            h, pair = divmod(u, 2)
            nc.scalar.activation(
                out=rs[pair].rearrange("p i j -> p (i j)"), in_=bank[4 + pair][:],
                func=ACT.Abs_reciprocal_sqrt, scale=0.5, bias=0.25,
            )
            for i in range(2):
                t = 2 * pair + i
                nc.vector.scalar_tensor_tensor(
                    out=z_planes[h][:, t, :], in0=d0[pair][:, i, :], scalar=gain[:, t : t + 1],
                    in1=rs[pair][:, i, :], op0=ALU.mult, op1=ALU.mult,
                )

        def quantise_z(h):
            for c in range(2):
                weave(nc.vector.tensor_copy, z_woven[2 * h + c], z_planes[h][:, :, block(c)])
            for c in range(2):
                quantise(z_w[h][:, block(c)], z_s[h][:, block(c)], z_woven[2 * h + c])

        def scores(h):
            for c in range(2):
                for t in range(PACK):
                    nc.tensor.matmul_mx(
                        out=a_bank[2 * h + c][:, block(t)],
                        lhsT=cand_w[:, block(t)].bitcast(FP8X4),
                        lhsT_scale=cand_s[:, block(t)],
                        rhs=z_w[h][:, block(c)].bitcast(FP8X4),
                        rhs_scale=z_s[h][:, block(c)],
                        start=True,
                        stop=True,
                    )
                nc.vector.tensor_scalar(
                    out=aw[:, :, block(2 * h + c)], in0=a_bank[2 * h + c][:].rearrange("p (t j) -> p t j", t=PACK),
                    scalar1=0.0625, scalar2=None, op0=ALU.mult,
                )

        wb_w = sb("wb_w", [P, S], U32)
        wb_s = sb("wb_s", [P, S], U8)
        b_bank = [bank[6], bank[7], bank[0], bank[1]]

        def project(t):
            nc.tensor.matmul_mx(
                out=b_bank[t][:], lhsT=cb_w[:, block(t)].bitcast(FP8X4), lhsT_scale=cb_s[:, block(t)],
                rhs=wb_w[:].bitcast(FP8X4), rhs_scale=wb_s[:], start=True, stop=True,
            )

        def size(t):
            if t in (1,):
                plain = sb("b_plain%d" % t, [P, S], F32)
                nc.vector.tensor_copy(out=plain[:], in_=b_bank[t][:])
                nc.vector.scalar_tensor_tensor(out=ab[:, t, :], in0=b_bank[t][:], scalar=-1.0, in1=plain[:], op0=ALU.mult, op1=ALU.max)
            else:
                nc.scalar.activation(out=ab[:, t, :], in_=b_bank[t][:], func=ACT.Abs)

        root_pairs = []
        diff_all = [sb("diff%d" % i, [P, S], F32) for i in range(2)]
        inv_t = [sb("inv_t%d" % c, [P, S], F32) for c in range(4)]
        flat = "p i j -> p (i j)"
        gb_half = [sq[0][:].rearrange("p (t j) -> p t j", t=PACK), factors[1][:]]
        gb = [gb_half[c // 2][:, :, block(c % 2)] for c in range(4)]
        planes = [inv_t[c][:].rearrange("p (t j) -> p t j", t=PACK) for c in range(4)]
        ga_rows = [gb[1], gb[2], planes[1], planes[2]]
        res_rows = [sb("res%d" % c, [P, PACK, BLK], F32) for c in range(4)]
        res_w = [sb("res_w%d" % h, [P, HALF], U32) for h in range(2)]
        res_s = sb("res_s", [P, S], U8)
        out_rows = out_0.rearrange("(p t) j -> p t j", t=PACK)
        out_words = out_1[0].rearrange("p c r -> p (c r)").bitcast(I32)

        def fetch_b(h):
            for t in range(PACK):
                nc.scalar.activation(out=gb_half[h][:, t, :], in_=ab[:, t, :].indirect(entries("n4", HALF * h, HALF)), func=ACT.Copy)

        def denominator(c):
            for t in range(PACK):
                transpose_sum(bank[c][:, block(t)], ab[:, t, block(c)], gb[c][:, t, :])

        def invert(c):
            if c % 2 == 0:
                root_pairs.append(sb("roots%d" % c, [P, 2, S], F32, tag=("cand_w", "cand_s")[c // 2]))
            root = root_pairs[c // 2][:, c % 2, :]
            nc.scalar.activation(out=root, in_=bank[c][:], func=ACT.Abs_reciprocal_sqrt, bias=0.5)
            if c in ():
                nc.scalar.activation(out=inv_t[c][:], in_=root, func=ACT.Square)
            else:
                nc.vector.tensor_tensor(out=inv_t[c][:], in0=root, in1=root, op=ALU.mult)

        def turn_back(c):
            for t in range(PACK):
                nc.tensor.transpose(bank[c][:, block(t)], inv_t[c][:, block(t)], ident[:])

        def result(first, width, copy):
            c, lo = divmod(first, BLK)
            ga = ga_rows[c][:, :, lo : lo + width]
            diff = diff_all[c % 2][:, PACK * lo : PACK * (lo + width)].rearrange("p (t j) -> p t j", t=PACK)
            res = res_rows[c][:, :, lo : lo + width]
            res_woven = sb("res_woven%d" % first, [P, width, PACK], BF16)
            cols = slice(first, first + width)
            for t in range(PACK):
                nc.scalar.activation(out=ga[:, t, :], in_=aw[:, t, :].indirect(entries("n3", first, width)), func=ACT.Copy)
            nc.vector.scalar_tensor_tensor(
                out=diff[:], in0=a_bank[c][:].rearrange("p (t j) -> p t j", t=PACK)[:, :, lo : lo + width], scalar=0.0625,
                in1=ga[:], op0=ALU.mult, op1=ALU.subtract,
            )
            nc.vector.tensor_tensor(
                out=res, in0=bank[c][:].rearrange("p (t j) -> p t j", t=PACK)[:, :, lo : lo + width], in1=diff[:], op=ALU.mult
            )
            if lo + width == BLK:
                nc.sync.dma_start(out_rows[:, :, block(c)], res_rows[c][:])
            if copy is None:
                nc.gpsimd.tensor_copy(out=res_woven[:], in_=res.rearrange("p t j -> p j t"))
            else:
                weave(copy, res_woven, res)
            h, place = divmod(first, HALF)
            quantise(res_w[h][:, place : place + width], res_s[:, cols], res_woven)
            if place + width == HALF:
                nc.sync.dma_start(out_words[:, HALF * h : HALF * (h + 1)], res_w[h][:].bitcast(I32))

        fetch(0)
        fetch(1)
        sums(0)
        squares(0)
        fetch(2)
        sums(1)
        add_squares(0)
        cb_w, cb_s = pick_stationary("cb")
        for h in range(2):
            weave(nc.vector.tensor_copy, wb_woven[h], wb_raw[h][:])
        for h in range(2):
            quantise(wb_w[:, HALF * h : HALF * (h + 1)], wb_s[:, HALF * h : HALF * (h + 1)], wb_woven[h])
        project(0)
        project(1)
        normalise(0)
        squares(1)
        fetch(3)
        sums(2)
        add_squares(1)
        normalise(1)
        squares(2)
        sums(3)
        size(0)
        size(1)
        add_squares(2)
        squares(3)
        normalise(2)
        add_squares(3)
        normalise(3)
        quantise_z(0)
        quantise_z(1)
        for t in (2, 3):
            project(t)
            size(t)
        cand_w, cand_s = pick_stationary("cand")
        scores(0)
        fetch_b(0)
        denominator(0)
        scores(1)
        invert(0)
        denominator(1)
        fetch_b(1)
        invert(1)
        denominator(2)
        turn_back(0)
        result(0, 128, nc.vector.tensor_copy)
        invert(2)
        denominator(3)
        invert(3)
        turn_back(1)
        result(128, 128, nc.vector.tensor_copy)
        turn_back(2)
        result(256, 128, nc.scalar.copy)
        turn_back(3)
        result(384, 64, nc.scalar.copy)
        result(448, 64, nc.vector.tensor_copy)
        for q in range(4):
            (nc.sync, nc.scalar)[q % 2].dma_start(out_2[0, 4 * q : 4 * q + 4, :].bitcast(I32), res_s[32 * q : 32 * q + 4, :].bitcast(I32))
